import numpy as np
import ml_dtypes


def mxq(x, axis, fmt="e4m3"):
    dtype, down = {"e4m3": (ml_dtypes.float8_e4m3fn, 7), "e5m2": (ml_dtypes.float8_e5m2, 14)}[fmt]
    v = np.moveaxis(np.asarray(x, np.float32).astype(ml_dtypes.bfloat16).astype(np.float64), axis, -1)
    blocks = v.reshape(v.shape[:-1] + (-1, 32))
    amax = np.abs(blocks).max(-1, keepdims=True)
    byte = np.maximum(np.where(amax > 0, np.frexp(amax)[1] - 1 + 127, 0) - down, 1)
    scale = np.exp2(byte - 127.0)
    codes = (blocks / scale).astype(np.float32).astype(dtype).astype(np.float64)
    return np.moveaxis((codes * scale).reshape(v.shape), -1, axis)


WIDE = False


def mx_kscale(k):
    if not WIDE:
        return np.ones(k)
    levels = np.array([10, -10, 5, -5, 0])
    if k % 512:
        return np.exp2(np.random.permutation(np.resize(levels, k // 32))).repeat(32)
    a = np.empty((k // 512, 16))
    for p in range(k // 512):
        a[p, :8] = np.random.permutation(np.resize(levels, 8))
        for g in range(8):
            far = levels[np.abs(levels - a[p, g]) >= 10]
            a[p, g + 8] = far[np.random.randint(len(far))]
    return np.exp2(a.ravel()).repeat(32)


def f64(x):
    return np.asarray(x).astype(np.float64)


def striped(idx):
    return np.tile(idx.reshape(-1, 16).T, (8, 1)).astype(np.uint16)


def unstriped(offs):
    return offs[:16].T.reshape(-1).astype(np.int64)


def striped8(idx):
    return np.concatenate([x.reshape(-1, 16).T for x in idx]).astype(np.uint16)


def runs(offs, k):
    lists = np.stack([offs[16 * r : 16 * r + 16].T.reshape(-1) for r in range(8)]).astype(np.int64)
    return lists[np.arange(k) % 512 // 64]


def pack_weight(w):
    k, n = w.shape
    w = f64(np.asarray(w, np.float32).astype(ml_dtypes.bfloat16)).reshape(k // 32, 32, n)
    amax = np.abs(w).max(1)
    byte = np.clip(np.where(amax > 0, np.frexp(amax)[1] - 1 + 127 - 7, 1), 1, 254)
    scaled = (w * np.exp2(127.0 - byte)[:, None, :]).reshape(k, n).astype(np.float32)
    words = np.ascontiguousarray(scaled.reshape(k // 512, 128, 4, n).transpose(0, 1, 3, 2)).astype(ml_dtypes.float8_e4m3fn).view(np.uint8)
    return words, np.ascontiguousarray(byte.astype(np.uint8).reshape(k // 512, 16, n))


def unpack_weight(words, scales):
    g, p, n, _ = words.shape
    vals = np.ascontiguousarray(words).view(ml_dtypes.float8_e4m3fn).astype(np.float64) * np.repeat(np.exp2(scales.astype(np.float64) - 127.0), 8, axis=1)[..., None]
    return vals.transpose(0, 1, 3, 2).reshape(g * 512, n)


E2M1 = np.array([0.0, 0.5, 1.0, 1.5, 2.0, 3.0, 4.0, 6.0, -0.0, -0.5, -1.0, -1.5, -2.0, -3.0, -4.0, -6.0])


def pack_fp4(w):
    k, n = w.shape
    w = f64(np.asarray(w, np.float32).astype(ml_dtypes.bfloat16)).reshape(k // 32, 32, n)
    amax = np.abs(w).max(1)
    mant, ex = np.frexp(amax / 6.0)
    byte = np.clip(np.where(amax > 0, np.where(mant > 0.5, ex, ex - 1) + 127, 1), 1, 254)
    scaled = (w * np.exp2(127.0 - byte)[:, None, :]).reshape(k, n).astype(np.float32)
    c = np.ascontiguousarray(scaled.reshape(k // 512, 128, 4, n).transpose(0, 1, 3, 2)).astype(ml_dtypes.float4_e2m1fn).view(np.uint8) & 0xF
    words = (c[..., 0::2] | (c[..., 1::2] << 4)).reshape(k // 512, 128, 2 * n)
    return np.ascontiguousarray(words), np.ascontiguousarray(byte.astype(np.uint8).reshape(k // 512, 16, n))


def unpack_fp4(words, scales):
    g, _, n = scales.shape
    words = np.ascontiguousarray(words).reshape(g, 128, n, 2)
    nib = np.empty((g, 128, n, 4), np.uint8)
    nib[..., 0::2] = words & 0xF
    nib[..., 1::2] = words >> 4
    vals = E2M1[nib] * np.repeat(np.exp2(scales.astype(np.float64) - 127.0), 8, axis=1)[..., None]
    return vals.transpose(0, 1, 3, 2).reshape(g * 512, n)


def sigmoid(v):
    return 1.0 / (1.0 + np.exp(-np.maximum(v, -700.0)))

def planes(y):
    n, m = y.shape
    v = y.astype(np.float32).astype(ml_dtypes.bfloat16).astype(np.float64).reshape(n // 32, 32, m)
    top = np.abs(v).max(1)
    byte = np.clip(np.where(top > 0, np.frexp(top)[1] - 1 + 127 - 7, 1), 1, 254)
    codes = (v * np.exp2(127.0 - byte)[:, None, :]).reshape(n, m).astype(np.float32).astype(ml_dtypes.float8_e4m3fn).view(np.uint8)
    words = codes.reshape(n // 512, 128, 4, m).transpose(0, 1, 3, 2)
    return np.ascontiguousarray(words), np.ascontiguousarray(byte.astype(np.uint8).reshape(n // 512, 16, m))


K, T, S, N, G, H, W = 512, 1024, 512, 512, 2048, 512, 384


def setup_inputs():
    n = np.random.standard_normal
    s = mx_kscale(K)[:, None]
    u = mx_kscale(S)
    packed_xT = pack_weight(n((K, T)) * s)
    packed_dT = pack_weight(n((K, G)) / s)
    packed_w1 = pack_fp4(n((H, N)) / np.sqrt(2 * H) / u[:, None])
    packed_w2 = pack_fp4(n((H, N)) / np.sqrt(2 * H) / u[:, None])
    return {
        "x_words": packed_xT[0],
        "x_scales": packed_xT[1],
        "d_words": packed_dT[0],
        "d_scales": packed_dT[1],
        "gn": (np.random.uniform(0.5, 1.5, (H, 1)) * u[:, None]).astype(np.float32),
        "gm": (np.random.uniform(0.5, 1.5, (H, 1)) * u[:, None]).astype(np.float32),
        "w1_words": packed_w1[0],
        "w1_scales": packed_w1[1],
        "w2_words": packed_w2[0],
        "w2_scales": packed_w2[1],
        "offs": striped(np.random.permutation(T)[:S]),
        "k1": striped8(np.random.randint(0, G, (8, H))),
        "two": striped(np.random.permutation(T)[:S]),
        "n1": striped8(np.stack([np.random.permutation(S) for _ in range(8)])),
        "n2": striped8(np.stack([np.random.permutation(S) for _ in range(8)])),
        "n3": striped(np.random.permutation(S)[:W]),
        "n4": striped(np.random.permutation(S)[:W]),
        "n5": striped8(np.stack([np.random.permutation(S) for _ in range(8)])),
        "n6": striped8(np.stack([np.random.permutation(S) for _ in range(8)])),
    }


def reference(x_words, x_scales, d_words, d_scales, gn, gm, w1_words, w1_scales, w2_words, w2_scales, offs, k1, two, n1, n2, n3, n4, n5, n6):
    d_k1 = unpack_weight(d_words, d_scales)[np.arange(K)[:, None], runs(k1, K)]
    xq = unpack_weight(x_words, x_scales)[:, unstriped(offs)]
    a = 0.0625 * (d_k1.T @ xq)
    z = f64(gn) * (a[np.arange(H)[:, None], runs(n1, H)] + 0.75 * (a[np.arange(H)[:, None], runs(n2, H)]))
    x_two = unpack_weight(x_words, x_scales)[:, unstriped(two)]
    b = 0.0625 * (d_k1.T @ x_two)
    old = b[:, unstriped(n3)]
    pa = b[:, unstriped(n4)]
    ra = old * sigmoid(pa)
    ds = b.copy()
    ds[:, unstriped(n3)] = ra
    z2 = f64(gm) * ds
    h = unpack_fp4(w1_words, w1_scales).T @ mxq(z, 0, "e4m3") + unpack_fp4(w2_words, w2_scales).T @ mxq(z2, 0, "e4m3")
    out_0 = 0.75 * (h[np.arange(N)[:, None], runs(n5, N)] + h[np.arange(N)[:, None], runs(n6, N)]) - h
    return (out_0,) + planes(out_0)

@@ -1,0 +1,243 @@
+from contextlib import ExitStack
+
+import concourse.mybir as mybir
+
+K, T, S, N, G, H, W = 512, 1024, 512, 512, 2048, 512, 384
+FLOPS = 4 * 2 * 512 * 512 * 512
+
+F32 = mybir.dt.float32
+BF16 = mybir.dt.bfloat16
+I32 = mybir.dt.int32
+U32 = mybir.dt.uint32
+U16 = mybir.dt.uint16
+U8 = mybir.dt.uint8
+FP8X4 = mybir.dt.float8_e4m3fn_x4
+FP4X4 = mybir.dt.float4_e2m1fn_x4
+ALU = mybir.AluOpType
+ACT = mybir.ActivationFunctionType
+
+P = 128
+PACK = 4
+HALF = S // 2
+LIST = 16
+WHOLE = ((0, S),)
+HALVED = ((0, HALF), (HALF, HALF))
+PIECES = (HALVED, WHOLE, WHOLE, HALVED)
+
+
+def tile_picked_kjsumkgatelap_none_po_kernel(
+    tc, x_words, x_scales, d_words, d_scales, gn, gm, w1_words, w1_scales, w2_words, w2_scales,
+    offs, k1, two, n1, n2, n3, n4, n5, n6, out_0, out_1, out_2,
+):
+    nc = tc.nc
+
+    with ExitStack() as ctx:
+        keep = ctx.enter_context(tc.tile_pool(name="keep", bufs=1))
+        psum = ctx.enter_context(tc.psum_pool(name="psum", bufs=1))
+
+        def sb(name, shape, dtype):
+            return keep.tile(shape, dtype, name=name, align_bytes=64)
+
+        def load_list(name, src):
+            tile = sb(name, list(src.shape), U16)
+            nc.sync.dma_start(tile[:], src)
+            return tile
+
+        def entries(tile, first, count):
+            return tile[:, first // LIST : (first + count) // LIST]
+
+        def deal(copy, dst, src, run):
+            copy(dst.rearrange("p (t c i) -> p c t i", t=PACK, i=run), src.rearrange("p (c i t) -> p c t i", t=PACK, i=run))
+
+        def load_plane(queue, tile_cols, scales):
+            for j in range(4):
+                queue.dma_start(tile_cols[j:P:32, :].bitcast(I32), scales[0, j:16:4, :].bitcast(I32))
+
+        d_scale_table = sb("d_scale_table", [P, G], U8)
+        x_scale_table = sb("x_scale_table", [P, T], U8)
+        nc.gpsimd.memset(x_scale_table[:].bitcast(I32), 0)
+        k1_l = load_list("k1_l", k1)
+        for j in range(2):
+            spread = d_scales[0, j:16:2, :].bitcast(I32).unsqueeze(1).to_broadcast([8, 8, G // 4])
+            nc.sync.dma_start(d_scale_table[j:P:2, :].bitcast(I32), spread)
+        two_l = load_list("two_l", two)
+        d_word_table = sb("d_word_table", [P, G], I32)
+        nc.sync.dma_start(d_word_table[:], d_words[0].rearrange("p n t -> p (n t)").bitcast(I32))
+        x_word_table = sb("x_word_table", [P, T], I32)
+        nc.sync.dma_start(x_word_table[:], x_words[0].rearrange("p n t -> p (n t)").bitcast(I32))
+        load_plane(nc.sync, x_scale_table, x_scales)
+
+        key_scales_picked = sb("key_scales_picked", [P, H], U8)
+        nc.vector.tensor_copy(key_scales_picked[:], d_scale_table[:].indirect(k1_l[:]))
+        key_scales_dealt = sb("key_scales_dealt", [P, H], U8)
+        deal(nc.vector.tensor_copy, key_scales_dealt[:], key_scales_picked[:], 16)
+        key_plane = sb("key_plane", [P, H], U8)
+        nc.gpsimd.memset(key_plane[:].bitcast(I32), 0)
+        nc.scalar.dma_start(key_plane[0:112, :].bitcast(I32), key_scales_dealt[14:126, :].bitcast(I32))
+
+        w_words = sb("w_words", [P, 2, N], U16)
+        for w, words in enumerate((w1_words, w2_words)):
+            raw = sb(f"w_words_raw{w}", [P, 2 * N], U8)
+            nc.sync.dma_start(raw[:].bitcast(I32), words[0].bitcast(I32))
+            deal(nc.scalar.copy, w_words[:, w, :], raw[:].bitcast(U16), 8)
+        offs_l = load_list("offs_l", offs)
+
+        def pick_token_scales(name, lst):
+            plane = sb(name, [P, S], U8)
+            nc.vector.tensor_copy(plane[:], x_scale_table[:].indirect(lst[:]))
+            return plane
+
+        def pick_token_words(name, lst):
+            words = sb(name, [P, S], U32)
+            nc.vector.tensor_copy(words[:], x_word_table[:].bitcast(U32).indirect(lst[:]))
+            return words
+
+        two_plane = pick_token_scales("two_plane", two_l)
+        key_words_picked = sb("key_words_picked", [P, H], U32)
+        nc.vector.tensor_copy(key_words_picked[:], d_word_table[:].bitcast(U32).indirect(k1_l[:]))
+        key_words = sb("key_words", [P, H], U32)
+        deal(nc.vector.tensor_copy, key_words[:], key_words_picked[:], 4)
+        two_words = pick_token_words("two_words", two_l)
+
+        n4_l = load_list("n4_l", n4)
+        n3_l = load_list("n3_l", n3)
+        gm_t = sb("gm_t", [P, PACK], F32)
+        nc.sync.dma_start(gm_t[:], gm.rearrange("(p t) o -> p (t o)", t=PACK))
+        gn_t = sb("gn_t", [P, PACK], F32)
+        nc.sync.dma_start(gn_t[:], gn.rearrange("(p t) o -> p (t o)", t=PACK))
+        gn_16th = sb("gn_16th", [P, PACK], F32)
+        nc.gpsimd.tensor_scalar(gn_16th[:], gn_t[:], 0.0625, 0.0, ALU.mult, ALU.add)
+        n2_l = load_list("n2_l", n2)
+        n1_l = load_list("n1_l", n1)
+
+        def scores(tag, words, plane):
+            banks = []
+            for t in range(PACK):
+                bank = psum.tile([P, S], F32, name=f"{tag}{t}", tag=f"{tag}{t}")
+                cols = slice(t * P, (t + 1) * P)
+                nc.tensor.matmul_mx(
+                    out=bank[:], lhsT=key_words[:, cols].bitcast(FP8X4), lhsT_scale=key_plane[:, cols],
+                    rhs=words[:].bitcast(FP8X4), rhs_scale=plane[:], start=True, stop=True,
+                )
+                banks.append(bank)
+            return banks
+
+        b_banks = scores("left", two_words, two_plane)
+        idx_plane = pick_token_scales("idx_plane", offs_l)
+        idx_words = pick_token_words("idx_words", offs_l)
+        a_banks = scores("right", idx_words, idx_plane)
+
+        w_scales_raw = sb("w_scales_raw", [P, 2, N], U8)
+        nc.gpsimd.memset(w_scales_raw[:].rearrange("p w n -> p (w n)").bitcast(I32), 0)
+        w_plane = sb("w_plane", [P, 2, N], U8)
+        for w, scales in enumerate((w1_scales, w2_scales)):
+            load_plane(nc.sync, w_scales_raw[:, w, :], scales)
+            deal(nc.gpsimd.tensor_copy, w_plane[:, w, :], w_scales_raw[:, w, :], 16)
+        n5_l = load_list("n5_l", n5)
+        n6_l = load_list("n6_l", n6)
+
+        def window(name, width):
+            tile = sb(name, [P, width], F32)
+            nc.gpsimd.memset(tile[:, S:], 0.0)
+            return tile
+
+        def weave(copy, woven, rows):
+            planes = rows.shape[1]
+            copy(woven.rearrange("p (c i t) -> p c t i", t=PACK, i=4)[:, :, :planes, :], rows.rearrange("p t (c i) -> p c t i", i=4))
+
+        def quantise(name, woven, plane):
+            words = sb(name, [P, plane.shape[1]], I32)
+            nc.vector.quantize_mx(out=words[:].bitcast(FP8X4), scales=plane, in_=woven)
+            return words
+
+        ds = [window(f"ds{t}", 2 * W) for t in range(PACK)]
+        rows = [window(f"rows{t}", 2 * S) for t in range(PACK)]
+        ra = [sb(f"ra{t}", [P, W], F32) for t in range(PACK)]
+        z_rows = sb("z_rows", [P, PACK, S], F32)
+        z2_rows = sb("z2_rows", [P, PACK - 1, S], BF16)
+        z2_woven = sb("z2_woven", [P, PACK * S], BF16)
+
+        def gate_columns(tiles):
+            for t in tiles:
+                nc.scalar.activation(ds[t][:, :S], b_banks[t][:], ACT.Copy, scale=0.0625)
+            for t in tiles:
+                gate = sb(f"gate{t}", [P, W], F32)
+                nc.scalar.activation(gate[:], ds[t][:].indirect(n4_l[:]), ACT.Sigmoid)
+                nc.vector.tensor_tensor(ra[t][:], ds[t][:].indirect(n3_l[:]), gate[:], ALU.mult)
+
+        def put_back(t):
+            nc.scalar.activation(ds[t][:].indirect(n3_l[:]), ra[t][:], ACT.Copy)
+            gain = gm_t[:, t : t + 1]
+            if t < PACK - 1:
+                nc.vector.tensor_scalar(z2_rows[:, t, :], ds[t][:, :S], gain, None, ALU.mult)
+            else:
+                nc.vector.tensor_scalar(z2_woven[:, t::PACK], ds[t][:, :S], gain, None, ALU.mult)
+
+        def mix_neighbours(t):
+            nc.scalar.activation(rows[t][:, :S], a_banks[t][:], ACT.Copy, scale=gn_16th[:, t : t + 1])
+            second = sb(f"second{t}", [P, S], F32)
+            nc.vector.tensor_scalar(second[:], rows[t][:].indirect(n2_l[:]), 0.75, 0.0, ALU.mult, ALU.add)
+            nc.vector.tensor_tensor(z_rows[:, t, :], rows[t][:].indirect(n1_l[:]), second[:], ALU.add)
+
+        def finish_z(half, copy):
+            woven = sb(f"z_woven{half}", [P, PACK * HALF], BF16)
+            weave(copy, woven[:], z_rows[:, :, half * HALF : (half + 1) * HALF])
+            plane = sb(f"z_plane{half}", [P, HALF], U8)
+            return quantise(f"z_words{half}", woven[:], plane[:]), plane
+
+        gate_columns((0, 1))
+        mix_neighbours(0)
+        mix_neighbours(1)
+        put_back(0)
+        gate_columns((2, 3))
+        mix_neighbours(2)
+        put_back(1)
+        mix_neighbours(3)
+        put_back(2)
+        z_first = finish_z(0, nc.vector.tensor_copy)
+        weave(nc.vector.tensor_copy, z2_woven[:], z2_rows[:])
+        put_back(3)
+        z2_plane = sb("z2_plane", [P, S], U8)
+        z2_words = quantise("z2_words", z2_woven[:], z2_plane[:])
+        z_second = finish_z(1, nc.scalar.copy)
+
+        h_banks = [psum.tile([P, S], F32, name=f"h{t}", tag=f"left{t}") for t in range(PACK)]
+
+        def weights_pass(w, t, cols, words, plane, start=False, stop=False):
+            keys = slice(t * P, (t + 1) * P)
+            nc.tensor.matmul_mx(
+                out=h_banks[t][:, cols], lhsT=w_words[:, w, keys].bitcast(FP4X4),
+                lhsT_scale=w_plane[:, w, keys], rhs=words[:].bitcast(FP8X4), rhs_scale=plane[:], start=start, stop=stop,
+            )
+
+        halves = (slice(0, HALF), slice(HALF, S))
+        for t in range(PACK):
+            weights_pass(0, t, halves[0], *z_first, start=True)
+        for t in range(PACK):
+            weights_pass(0, t, halves[1], *z_second)
+        for t in range(PACK):
+            weights_pass(1, t, slice(0, S), z2_words, z2_plane, stop=True)
+
+        out_rows_hbm = out_0.rearrange("(p t) j -> p t j", t=PACK)
+        out_words_hbm = out_1[0].rearrange("p n t -> p (n t)").bitcast(I32)
+        out_plane = sb("out_plane", [P, S], U8)
+        out_rows = sb("out_rows", [P, PACK, S], F32)
+        for t in range(PACK):
+            copy = nc.vector.tensor_copy if t == 1 else nc.scalar.copy
+            copy(rows[t][:, :S], h_banks[t][:])
+            for first, count in PIECES[t]:
+                cols = slice(first, first + count)
+                fifth = sb(f"fifth{t}_{first}", [P, count], F32)
+                nc.scalar.activation(fifth[:], rows[t][:].indirect(entries(n5_l, first, count)), ACT.Copy)
+                both = sb(f"both{t}_{first}", [P, count], F32)
+                nc.vector.tensor_tensor(both[:], rows[t][:].indirect(entries(n6_l, first, count)), fifth[:], ALU.add)
+                nc.vector.scalar_tensor_tensor(out_rows[:, t, cols], both[:], 0.75, h_banks[t][:, cols], ALU.mult, ALU.subtract)
+            nc.sync.dma_start(out_rows_hbm[:, t, :], out_rows[:, t, :])
+        for half, copy in enumerate((nc.scalar.copy, nc.vector.tensor_copy)):
+            cols = halves[half]
+            out_woven = sb(f"out_woven{half}", [P, PACK * HALF], BF16)
+            weave(copy, out_woven[:], out_rows[:, :, cols])
+            out_words = quantise(f"out_words{half}", out_woven[:], out_plane[:, cols])
+            nc.sync.dma_start(out_words_hbm[:, cols], out_words[:])
+        for j in range(4):
+            nc.scalar.dma_start(out_2[0, j:16:4, :].bitcast(I32), out_plane[j:P:32, :].bitcast(I32))

@@ -20,9 +20,7 @@ P = 128
 PACK = 4
 HALF = S // 2
 LIST = 16
-WHOLE = ((0, S),)
-HALVED = ((0, HALF), (HALF, HALF))
-PIECES = (HALVED, WHOLE, WHOLE, HALVED)
+V_EVAC = ((0, 1), (1, 0), (1, 1))
 
 
 def tile_picked_kjsumkgatelap_none_po_kernel(
@@ -43,8 +41,10 @@ def tile_picked_kjsumkgatelap_none_po_kernel(
             nc.sync.dma_start(tile[:], src)
             return tile
 
-        def entries(tile, first, count):
-            return tile[:, first // LIST : (first + count) // LIST]
+        halves = (slice(0, HALF), slice(HALF, S))
+
+        def entries(tile, cols):
+            return tile[:, cols.start // LIST : cols.stop // LIST]
 
         def deal(copy, dst, src, run):
             copy(dst.rearrange("p (t c i) -> p c t i", t=PACK, i=run), src.rearrange("p (c i t) -> p c t i", t=PACK, i=run))
@@ -61,10 +61,14 @@ def tile_picked_kjsumkgatelap_none_po_kernel(
             spread = d_scales[0, j:16:2, :].bitcast(I32).unsqueeze(1).to_broadcast([8, 8, G // 4])
             nc.sync.dma_start(d_scale_table[j:P:2, :].bitcast(I32), spread)
         two_l = load_list("two_l", two)
-        d_word_table = sb("d_word_table", [P, G], I32)
-        nc.sync.dma_start(d_word_table[:], d_words[0].rearrange("p n t -> p (n t)").bitcast(I32))
+        gn_t = sb("gn_t", [P, PACK], F32)
+        nc.sync.dma_start(gn_t[:], gn.rearrange("(p t) o -> p (t o)", t=PACK))
+        gn_16th = sb("gn_16th", [P, PACK], F32)
+        nc.scalar.activation(gn_16th[:], gn_t[:], ACT.Copy, scale=0.0625)
         x_word_table = sb("x_word_table", [P, T], I32)
         nc.sync.dma_start(x_word_table[:], x_words[0].rearrange("p n t -> p (n t)").bitcast(I32))
+        d_word_table = sb("d_word_table", [P, G], I32)
+        nc.sync.dma_start(d_word_table[:], d_words[0].rearrange("p n t -> p (n t)").bitcast(I32))
         load_plane(nc.sync, x_scale_table, x_scales)
 
         key_scales_picked = sb("key_scales_picked", [P, H], U8)
@@ -103,10 +107,6 @@ def tile_picked_kjsumkgatelap_none_po_kernel(
         n3_l = load_list("n3_l", n3)
         gm_t = sb("gm_t", [P, PACK], F32)
         nc.sync.dma_start(gm_t[:], gm.rearrange("(p t) o -> p (t o)", t=PACK))
-        gn_t = sb("gn_t", [P, PACK], F32)
-        nc.sync.dma_start(gn_t[:], gn.rearrange("(p t) o -> p (t o)", t=PACK))
-        gn_16th = sb("gn_16th", [P, PACK], F32)
-        nc.gpsimd.tensor_scalar(gn_16th[:], gn_t[:], 0.0625, 0.0, ALU.mult, ALU.add)
         n2_l = load_list("n2_l", n2)
         n1_l = load_list("n1_l", n1)
 
@@ -136,9 +136,9 @@ def tile_picked_kjsumkgatelap_none_po_kernel(
         n5_l = load_list("n5_l", n5)
         n6_l = load_list("n6_l", n6)
 
-        def window(name, width):
+        def window(name, width, engine):
             tile = sb(name, [P, width], F32)
-            nc.gpsimd.memset(tile[:, S:], 0.0)
+            engine.memset(tile[:, S:], 0.0)
             return tile
 
         def weave(copy, woven, rows):
@@ -150,20 +150,20 @@ def tile_picked_kjsumkgatelap_none_po_kernel(
             nc.vector.quantize_mx(out=words[:].bitcast(FP8X4), scales=plane, in_=woven)
             return words
 
-        ds = [window(f"ds{t}", 2 * W) for t in range(PACK)]
-        rows = [window(f"rows{t}", 2 * S) for t in range(PACK)]
+        ds = [window(f"ds{t}", 2 * W, nc.gpsimd) for t in range(PACK)]
+        rows = [window(f"rows{t}", 2 * S, nc.vector) for t in range(PACK)]
         ra = [sb(f"ra{t}", [P, W], F32) for t in range(PACK)]
         z_rows = sb("z_rows", [P, PACK, S], F32)
         z2_rows = sb("z2_rows", [P, PACK - 1, S], BF16)
         z2_woven = sb("z2_woven", [P, PACK * S], BF16)
 
-        def gate_columns(tiles):
-            for t in tiles:
-                nc.scalar.activation(ds[t][:, :S], b_banks[t][:], ACT.Copy, scale=0.0625)
-            for t in tiles:
-                gate = sb(f"gate{t}", [P, W], F32)
-                nc.scalar.activation(gate[:], ds[t][:].indirect(n4_l[:]), ACT.Sigmoid)
-                nc.vector.tensor_tensor(ra[t][:], ds[t][:].indirect(n3_l[:]), gate[:], ALU.mult)
+        def take_b(t):
+            nc.scalar.activation(ds[t][:, :S], b_banks[t][:], ACT.Copy, scale=0.0625)
+
+        def gate_columns(t):
+            gate = sb(f"gate{t}", [P, W], F32)
+            nc.scalar.activation(gate[:], ds[t][:].indirect(n4_l[:]), ACT.Sigmoid)
+            nc.vector.tensor_tensor(ra[t][:], ds[t][:].indirect(n3_l[:]), gate[:], ALU.mult)
 
         def put_back(t):
             nc.scalar.activation(ds[t][:].indirect(n3_l[:]), ra[t][:], ACT.Copy)
@@ -176,8 +176,10 @@ def tile_picked_kjsumkgatelap_none_po_kernel(
         def mix_neighbours(t):
             nc.scalar.activation(rows[t][:, :S], a_banks[t][:], ACT.Copy, scale=gn_16th[:, t : t + 1])
             second = sb(f"second{t}", [P, S], F32)
-            nc.vector.tensor_scalar(second[:], rows[t][:].indirect(n2_l[:]), 0.75, 0.0, ALU.mult, ALU.add)
-            nc.vector.tensor_tensor(z_rows[:, t, :], rows[t][:].indirect(n1_l[:]), second[:], ALU.add)
+            for cols in halves:
+                nc.vector.tensor_scalar(second[:, cols], rows[t][:].indirect(entries(n2_l, cols)), 0.75, 0.0, ALU.mult, ALU.add)
+            for cols in halves:
+                nc.vector.tensor_tensor(z_rows[:, t, cols], rows[t][:].indirect(entries(n1_l, cols)), second[:, cols], ALU.add)
 
         def finish_z(half, copy):
             woven = sb(f"z_woven{half}", [P, PACK * HALF], BF16)
@@ -185,15 +187,14 @@ def tile_picked_kjsumkgatelap_none_po_kernel(
             plane = sb(f"z_plane{half}", [P, HALF], U8)
             return quantise(f"z_words{half}", woven[:], plane[:]), plane
 
-        gate_columns((0, 1))
-        mix_neighbours(0)
-        mix_neighbours(1)
-        put_back(0)
-        gate_columns((2, 3))
-        mix_neighbours(2)
-        put_back(1)
-        mix_neighbours(3)
-        put_back(2)
+        take_b(0)
+        for t in range(PACK):
+            if t + 1 < PACK:
+                take_b(t + 1)
+            gate_columns(t)
+            mix_neighbours(t)
+            if t > 0:
+                put_back(t - 1)
         z_first = finish_z(0, nc.vector.tensor_copy)
         weave(nc.vector.tensor_copy, z2_woven[:], z2_rows[:])
         put_back(3)
@@ -201,37 +202,40 @@ def tile_picked_kjsumkgatelap_none_po_kernel(
         z2_words = quantise("z2_words", z2_woven[:], z2_plane[:])
         z_second = finish_z(1, nc.scalar.copy)
 
-        h_banks = [psum.tile([P, S], F32, name=f"h{t}", tag=f"left{t}") for t in range(PACK)]
+        h_banks = [
+            [psum.tile([P, HALF], F32, name=f"h{t}_{side}", tag=f"{side}{t}") for side in ("left", "right")] for t in range(PACK)
+        ]
 
-        def weights_pass(w, t, cols, words, plane, start=False, stop=False):
+        def weights_pass(w, t, half, words, plane):
             keys = slice(t * P, (t + 1) * P)
             nc.tensor.matmul_mx(
-                out=h_banks[t][:, cols], lhsT=w_words[:, w, keys].bitcast(FP4X4),
-                lhsT_scale=w_plane[:, w, keys], rhs=words[:].bitcast(FP8X4), rhs_scale=plane[:], start=start, stop=stop,
+                out=h_banks[t][half][:], lhsT=w_words[:, w, keys].bitcast(FP4X4), lhsT_scale=w_plane[:, w, keys],
+                rhs=words.bitcast(FP8X4), rhs_scale=plane, start=w == 0, stop=w == 1,
             )
 
-        halves = (slice(0, HALF), slice(HALF, S))
         for t in range(PACK):
-            weights_pass(0, t, halves[0], *z_first, start=True)
+            weights_pass(0, t, 0, z_first[0][:], z_first[1][:])
         for t in range(PACK):
-            weights_pass(0, t, halves[1], *z_second)
-        for t in range(PACK):
-            weights_pass(1, t, slice(0, S), z2_words, z2_plane, stop=True)
+            weights_pass(0, t, 1, z_second[0][:], z_second[1][:])
+            for half, cols in enumerate(halves):
+                weights_pass(1, t, half, z2_words[:, cols], z2_plane[:, cols])
 
         out_rows_hbm = out_0.rearrange("(p t) j -> p t j", t=PACK)
         out_words_hbm = out_1[0].rearrange("p n t -> p (n t)").bitcast(I32)
         out_plane = sb("out_plane", [P, S], U8)
         out_rows = sb("out_rows", [P, PACK, S], F32)
         for t in range(PACK):
-            copy = nc.vector.tensor_copy if t == 1 else nc.scalar.copy
-            copy(rows[t][:, :S], h_banks[t][:])
-            for first, count in PIECES[t]:
-                cols = slice(first, first + count)
-                fifth = sb(f"fifth{t}_{first}", [P, count], F32)
-                nc.scalar.activation(fifth[:], rows[t][:].indirect(entries(n5_l, first, count)), ACT.Copy)
-                both = sb(f"both{t}_{first}", [P, count], F32)
-                nc.vector.tensor_tensor(both[:], rows[t][:].indirect(entries(n6_l, first, count)), fifth[:], ALU.add)
-                nc.vector.scalar_tensor_tensor(out_rows[:, t, cols], both[:], 0.75, h_banks[t][:, cols], ALU.mult, ALU.subtract)
+            for half, cols in enumerate(halves):
+                copy = nc.vector.tensor_copy if (t, half) in V_EVAC else nc.scalar.copy
+                copy(rows[t][:, cols], h_banks[t][half][:])
+            fifth = sb(f"fifth{t}", [P, S], F32)
+            both = sb(f"both{t}", [P, S], F32)
+            for cols in halves if t == 0 else (slice(0, S),):
+                nc.scalar.activation(fifth[:, cols], rows[t][:].indirect(entries(n5_l, cols)), ACT.Copy)
+            for cols in halves:
+                nc.vector.tensor_tensor(both[:, cols], rows[t][:].indirect(entries(n6_l, cols)), fifth[:, cols], ALU.add)
+            for half, cols in enumerate(halves):
+                nc.vector.scalar_tensor_tensor(out_rows[:, t, cols], both[:, cols], 0.75, h_banks[t][half][:], ALU.mult, ALU.subtract)
             nc.sync.dma_start(out_rows_hbm[:, t, :], out_rows[:, t, :])
         for half, copy in enumerate((nc.scalar.copy, nc.vector.tensor_copy)):
             cols = halves[half]

@@ -53,37 +53,47 @@ def tile_picked_kjsumkgatelap_none_po_kernel(
             for j in range(4):
                 queue.dma_start(tile_cols[j:P:32, :].bitcast(I32), scales[0, j:16:4, :].bitcast(I32))
 
+        def load_by_runs(tile, scales):
+            for j in range(2):
+                spread = scales[0, j:16:2, :].bitcast(I32).unsqueeze(1).to_broadcast([8, 8, scales.shape[2] // 4])
+                nc.sync.dma_start(tile[j:P:2, :].bitcast(I32), spread)
+
+        def shift_to_plane(name, dealt):
+            plane = sb(name, list(dealt.shape), U8)
+            nc.gpsimd.memset(plane[:].bitcast(I32), 0)
+            nc.scalar.dma_start(plane[0:112, :].bitcast(I32), dealt[14:126, :].bitcast(I32))
+            return plane
+
+        warm = sb("warm", [P, 2], F32)
+        nc.gpsimd.memset(warm[:, 0:1], 0.0)
+        nc.scalar.activation(warm[:, 1:2], warm[:, 0:1], ACT.Sigmoid)
+
         d_scale_table = sb("d_scale_table", [P, G], U8)
         x_scale_table = sb("x_scale_table", [P, T], U8)
         nc.gpsimd.memset(x_scale_table[:].bitcast(I32), 0)
         k1_l = load_list("k1_l", k1)
-        for j in range(2):
-            spread = d_scales[0, j:16:2, :].bitcast(I32).unsqueeze(1).to_broadcast([8, 8, G // 4])
-            nc.sync.dma_start(d_scale_table[j:P:2, :].bitcast(I32), spread)
+        load_by_runs(d_scale_table[:], d_scales)
         two_l = load_list("two_l", two)
-        gn_t = sb("gn_t", [P, PACK], F32)
-        nc.sync.dma_start(gn_t[:], gn.rearrange("(p t) o -> p (t o)", t=PACK))
-        gn_16th = sb("gn_16th", [P, PACK], F32)
-        nc.scalar.activation(gn_16th[:], gn_t[:], ACT.Copy, scale=0.0625)
+        n4_l = load_list("n4_l", n4)
+        n3_l = load_list("n3_l", n3)
         x_word_table = sb("x_word_table", [P, T], I32)
         nc.sync.dma_start(x_word_table[:], x_words[0].rearrange("p n t -> p (n t)").bitcast(I32))
         d_word_table = sb("d_word_table", [P, G], I32)
         nc.sync.dma_start(d_word_table[:], d_words[0].rearrange("p n t -> p (n t)").bitcast(I32))
         load_plane(nc.sync, x_scale_table, x_scales)
 
-        key_scales_picked = sb("key_scales_picked", [P, H], U8)
-        nc.vector.tensor_copy(key_scales_picked[:], d_scale_table[:].indirect(k1_l[:]))
-        key_scales_dealt = sb("key_scales_dealt", [P, H], U8)
-        deal(nc.vector.tensor_copy, key_scales_dealt[:], key_scales_picked[:], 16)
-        key_plane = sb("key_plane", [P, H], U8)
-        nc.gpsimd.memset(key_plane[:].bitcast(I32), 0)
-        nc.scalar.dma_start(key_plane[0:112, :].bitcast(I32), key_scales_dealt[14:126, :].bitcast(I32))
-
         w_words = sb("w_words", [P, 2, N], U16)
         for w, words in enumerate((w1_words, w2_words)):
             raw = sb(f"w_words_raw{w}", [P, 2 * N], U8)
             nc.sync.dma_start(raw[:].bitcast(I32), words[0].bitcast(I32))
             deal(nc.scalar.copy, w_words[:, w, :], raw[:].bitcast(U16), 8)
+
+        key_scales_picked = sb("key_scales_picked", [P, H], U8)
+        nc.vector.tensor_copy(key_scales_picked[:], d_scale_table[:].indirect(k1_l[:]))
+        key_scales_dealt = sb("key_scales_dealt", [P, H], U8)
+        deal(nc.vector.tensor_copy, key_scales_dealt[:], key_scales_picked[:], 16)
+        key_plane = shift_to_plane("key_plane", key_scales_dealt)
+
         offs_l = load_list("offs_l", offs)
 
         def pick_token_scales(name, lst):
@@ -103,8 +113,10 @@ def tile_picked_kjsumkgatelap_none_po_kernel(
         deal(nc.vector.tensor_copy, key_words[:], key_words_picked[:], 4)
         two_words = pick_token_words("two_words", two_l)
 
-        n4_l = load_list("n4_l", n4)
-        n3_l = load_list("n3_l", n3)
+        gn_t = sb("gn_t", [P, PACK], F32)
+        nc.sync.dma_start(gn_t[:], gn.rearrange("(p t) o -> p (t o)", t=PACK))
+        gn_16th = sb("gn_16th", [P, PACK], F32)
+        nc.scalar.activation(gn_16th[:], gn_t[:], ACT.Copy, scale=0.0625)
         gm_t = sb("gm_t", [P, PACK], F32)
         nc.sync.dma_start(gm_t[:], gm.rearrange("(p t) o -> p (t o)", t=PACK))
         n2_l = load_list("n2_l", n2)
@@ -127,12 +139,13 @@ def tile_picked_kjsumkgatelap_none_po_kernel(
         idx_words = pick_token_words("idx_words", offs_l)
         a_banks = scores("right", idx_words, idx_plane)
 
-        w_scales_raw = sb("w_scales_raw", [P, 2, N], U8)
-        nc.gpsimd.memset(w_scales_raw[:].rearrange("p w n -> p (w n)").bitcast(I32), 0)
-        w_plane = sb("w_plane", [P, 2, N], U8)
+        w_scales_raw = sb("w_scales_raw", [P, 2 * N], U8)
+        w_scales_dealt = sb("w_scales_dealt", [P, 2 * N], U8)
         for w, scales in enumerate((w1_scales, w2_scales)):
-            load_plane(nc.sync, w_scales_raw[:, w, :], scales)
-            deal(nc.gpsimd.tensor_copy, w_plane[:, w, :], w_scales_raw[:, w, :], 16)
+            cols = slice(w * N, (w + 1) * N)
+            load_by_runs(w_scales_raw[:, cols], scales)
+            deal(nc.gpsimd.tensor_copy, w_scales_dealt[:, cols], w_scales_raw[:, cols], 16)
+        w_plane = shift_to_plane("w_plane", w_scales_dealt)
         n5_l = load_list("n5_l", n5)
         n6_l = load_list("n6_l", n6)
 
@@ -176,10 +189,8 @@ def tile_picked_kjsumkgatelap_none_po_kernel(
         def mix_neighbours(t):
             nc.scalar.activation(rows[t][:, :S], a_banks[t][:], ACT.Copy, scale=gn_16th[:, t : t + 1])
             second = sb(f"second{t}", [P, S], F32)
-            for cols in halves:
-                nc.vector.tensor_scalar(second[:, cols], rows[t][:].indirect(entries(n2_l, cols)), 0.75, 0.0, ALU.mult, ALU.add)
-            for cols in halves:
-                nc.vector.tensor_tensor(z_rows[:, t, cols], rows[t][:].indirect(entries(n1_l, cols)), second[:, cols], ALU.add)
+            nc.vector.tensor_scalar(second[:], rows[t][:].indirect(n2_l[:]), 0.75, 0.0, ALU.mult, ALU.add)
+            nc.vector.tensor_tensor(z_rows[:, t, :], rows[t][:].indirect(n1_l[:]), second[:], ALU.add)
 
         def finish_z(half, copy):
             woven = sb(f"z_woven{half}", [P, PACK * HALF], BF16)
@@ -209,7 +220,7 @@ def tile_picked_kjsumkgatelap_none_po_kernel(
         def weights_pass(w, t, half, words, plane):
             keys = slice(t * P, (t + 1) * P)
             nc.tensor.matmul_mx(
-                out=h_banks[t][half][:], lhsT=w_words[:, w, keys].bitcast(FP4X4), lhsT_scale=w_plane[:, w, keys],
+                out=h_banks[t][half][:], lhsT=w_words[:, w, keys].bitcast(FP4X4), lhsT_scale=w_plane[:, w * N + t * P : w * N + (t + 1) * P],
                 rhs=words.bitcast(FP8X4), rhs_scale=plane, start=w == 0, stop=w == 1,
             )
 
@@ -232,10 +243,19 @@ def tile_picked_kjsumkgatelap_none_po_kernel(
             both = sb(f"both{t}", [P, S], F32)
             for cols in halves if t == 0 else (slice(0, S),):
                 nc.scalar.activation(fifth[:, cols], rows[t][:].indirect(entries(n5_l, cols)), ACT.Copy)
-            for cols in halves:
-                nc.vector.tensor_tensor(both[:, cols], rows[t][:].indirect(entries(n6_l, cols)), fifth[:, cols], ALU.add)
-            for half, cols in enumerate(halves):
-                nc.vector.scalar_tensor_tensor(out_rows[:, t, cols], both[:, cols], 0.75, h_banks[t][half][:], ALU.mult, ALU.subtract)
+            if t < PACK - 1:
+                for cols in halves if t == 0 else (slice(0, S),):
+                    nc.vector.tensor_tensor(both[:, cols], rows[t][:].indirect(entries(n6_l, cols)), fifth[:, cols], ALU.add)
+                for half, cols in enumerate(halves):
+                    nc.vector.scalar_tensor_tensor(out_rows[:, t, cols], both[:, cols], 0.75, h_banks[t][half][:], ALU.mult, ALU.subtract)
+            else:
+                left, right = halves
+                sixth = sb("sixth", [P, HALF], F32)
+                nc.scalar.activation(sixth[:], rows[t][:].indirect(entries(n6_l, right)), ACT.Copy)
+                nc.vector.tensor_tensor(both[:, left], rows[t][:].indirect(entries(n6_l, left)), fifth[:, left], ALU.add)
+                nc.vector.scalar_tensor_tensor(both[:, right], fifth[:, right], 0.75, h_banks[t][1][:], ALU.mult, ALU.subtract)
+                nc.vector.scalar_tensor_tensor(out_rows[:, t, left], both[:, left], 0.75, h_banks[t][0][:], ALU.mult, ALU.subtract)
+                nc.vector.scalar_tensor_tensor(out_rows[:, t, right], sixth[:], 0.75, both[:, right], ALU.mult, ALU.add)
             nc.sync.dma_start(out_rows_hbm[:, t, :], out_rows[:, t, :])
         for half, copy in enumerate((nc.scalar.copy, nc.vector.tensor_copy)):
             cols = halves[half]

@@ -81,6 +81,7 @@ def tile_picked_kjsumkgatelap_none_po_kernel(
         d_word_table = sb("d_word_table", [P, G], I32)
         nc.sync.dma_start(d_word_table[:], d_words[0].rearrange("p n t -> p (n t)").bitcast(I32))
         load_plane(nc.sync, x_scale_table, x_scales)
+        offs_l = load_list("offs_l", offs)
 
         w_words = sb("w_words", [P, 2, N], U16)
         for w, words in enumerate((w1_words, w2_words)):
@@ -94,7 +95,6 @@ def tile_picked_kjsumkgatelap_none_po_kernel(
         deal(nc.vector.tensor_copy, key_scales_dealt[:], key_scales_picked[:], 16)
         key_plane = shift_to_plane("key_plane", key_scales_dealt)
 
-        offs_l = load_list("offs_l", offs)
 
         def pick_token_scales(name, lst):
             plane = sb(name, [P, S], U8)
@@ -171,7 +171,10 @@ def tile_picked_kjsumkgatelap_none_po_kernel(
         z2_woven = sb("z2_woven", [P, PACK * S], BF16)
 
         def take_b(t):
-            nc.scalar.activation(ds[t][:, :S], b_banks[t][:], ACT.Copy, scale=0.0625)
+            if t < 2:
+                nc.scalar.activation(ds[t][:, :S], b_banks[t][:], ACT.Copy, scale=0.0625)
+            else:
+                nc.vector.tensor_scalar(ds[t][:, :S], b_banks[t][:], 0.0625, None, ALU.mult)
 
         def gate_columns(t):
             gate = sb(f"gate{t}", [P, W], F32)
@@ -189,29 +192,29 @@ def tile_picked_kjsumkgatelap_none_po_kernel(
         def mix_neighbours(t):
             nc.scalar.activation(rows[t][:, :S], a_banks[t][:], ACT.Copy, scale=gn_16th[:, t : t + 1])
             second = sb(f"second{t}", [P, S], F32)
-            nc.vector.tensor_scalar(second[:], rows[t][:].indirect(n2_l[:]), 0.75, 0.0, ALU.mult, ALU.add)
-            nc.vector.tensor_tensor(z_rows[:, t, :], rows[t][:].indirect(n1_l[:]), second[:], ALU.add)
+            for cols in halves:
+                nc.vector.tensor_scalar(second[:, cols], rows[t][:].indirect(entries(n2_l, cols)), 0.75, 0.0, ALU.mult, ALU.add)
+            for cols in halves:
+                nc.vector.tensor_tensor(z_rows[:, t, cols], rows[t][:].indirect(entries(n1_l, cols)), second[:, cols], ALU.add)
 
-        def finish_z(half, copy):
+        def finish_z(half):
             woven = sb(f"z_woven{half}", [P, PACK * HALF], BF16)
-            weave(copy, woven[:], z_rows[:, :, half * HALF : (half + 1) * HALF])
+            weave(nc.scalar.copy, woven[:], z_rows[:, :, halves[half]])
             plane = sb(f"z_plane{half}", [P, HALF], U8)
             return quantise(f"z_words{half}", woven[:], plane[:]), plane
 
-        take_b(0)
         for t in range(PACK):
-            if t + 1 < PACK:
-                take_b(t + 1)
+            take_b(t)
+        for t in range(PACK):
             gate_columns(t)
             mix_neighbours(t)
             if t > 0:
                 put_back(t - 1)
-        z_first = finish_z(0, nc.vector.tensor_copy)
         weave(nc.vector.tensor_copy, z2_woven[:], z2_rows[:])
         put_back(3)
         z2_plane = sb("z2_plane", [P, S], U8)
         z2_words = quantise("z2_words", z2_woven[:], z2_plane[:])
-        z_second = finish_z(1, nc.scalar.copy)
+        z_halves = [finish_z(half) for half in range(2)]
 
         h_banks = [
             [psum.tile([P, HALF], F32, name=f"h{t}_{side}", tag=f"{side}{t}") for side in ("left", "right")] for t in range(PACK)
@@ -221,15 +224,14 @@ def tile_picked_kjsumkgatelap_none_po_kernel(
             keys = slice(t * P, (t + 1) * P)
             nc.tensor.matmul_mx(
                 out=h_banks[t][half][:], lhsT=w_words[:, w, keys].bitcast(FP4X4), lhsT_scale=w_plane[:, w * N + t * P : w * N + (t + 1) * P],
-                rhs=words.bitcast(FP8X4), rhs_scale=plane, start=w == 0, stop=w == 1,
+                rhs=words.bitcast(FP8X4), rhs_scale=plane, start=w == 1, stop=w == 0,
             )
 
         for t in range(PACK):
-            weights_pass(0, t, 0, z_first[0][:], z_first[1][:])
-        for t in range(PACK):
-            weights_pass(0, t, 1, z_second[0][:], z_second[1][:])
             for half, cols in enumerate(halves):
                 weights_pass(1, t, half, z2_words[:, cols], z2_plane[:, cols])
+            for half, (words, plane) in enumerate(z_halves):
+                weights_pass(0, t, half, words[:], plane[:])
 
         out_rows_hbm = out_0.rearrange("(p t) j -> p t j", t=PACK)
         out_words_hbm = out_1[0].rearrange("p n t -> p (n t)").bitcast(I32)
@@ -244,7 +246,7 @@ def tile_picked_kjsumkgatelap_none_po_kernel(
             for cols in halves if t == 0 else (slice(0, S),):
                 nc.scalar.activation(fifth[:, cols], rows[t][:].indirect(entries(n5_l, cols)), ACT.Copy)
             if t < PACK - 1:
-                for cols in halves if t == 0 else (slice(0, S),):
+                for cols in halves:
                     nc.vector.tensor_tensor(both[:, cols], rows[t][:].indirect(entries(n6_l, cols)), fifth[:, cols], ALU.add)
                 for half, cols in enumerate(halves):
                     nc.vector.scalar_tensor_tensor(out_rows[:, t, cols], both[:, cols], 0.75, h_banks[t][half][:], ALU.mult, ALU.subtract)

from contextlib import ExitStack

import concourse.mybir as mybir

K, T, S, N, G, H, W = 512, 1024, 512, 512, 2048, 512, 384
FLOPS = 4 * 2 * 512 * 512 * 512

F32 = mybir.dt.float32
BF16 = mybir.dt.bfloat16
I32 = mybir.dt.int32
U32 = mybir.dt.uint32
U16 = mybir.dt.uint16
U8 = mybir.dt.uint8
FP8X4 = mybir.dt.float8_e4m3fn_x4
FP4X4 = mybir.dt.float4_e2m1fn_x4
ALU = mybir.AluOpType
ACT = mybir.ActivationFunctionType

P = 128
PACK = 4
HALF = S // 2
LIST = 16
V_EVAC = ((0, 1), (1, 0), (1, 1))


def tile_picked_kjsumkgatelap_none_po_kernel(
    tc, x_words, x_scales, d_words, d_scales, gn, gm, w1_words, w1_scales, w2_words, w2_scales,
    offs, k1, two, n1, n2, n3, n4, n5, n6, out_0, out_1, out_2,
):
    nc = tc.nc

    with ExitStack() as ctx:
        keep = ctx.enter_context(tc.tile_pool(name="keep", bufs=1))
        psum = ctx.enter_context(tc.psum_pool(name="psum", bufs=1))

        def sb(name, shape, dtype):
            return keep.tile(shape, dtype, name=name, align_bytes=64)

        def load_list(name, src):
            tile = sb(name, list(src.shape), U16)
            nc.sync.dma_start(tile[:], src)
            return tile

        halves = (slice(0, HALF), slice(HALF, S))

        def entries(tile, cols):
            return tile[:, cols.start // LIST : cols.stop // LIST]

        def deal(copy, dst, src, run):
            copy(dst.rearrange("p (t c i) -> p c t i", t=PACK, i=run), src.rearrange("p (c i t) -> p c t i", t=PACK, i=run))

        def load_plane(queue, tile_cols, scales):
            for j in range(4):
                queue.dma_start(tile_cols[j:P:32, :].bitcast(I32), scales[0, j:16:4, :].bitcast(I32))

        def load_by_runs(tile, scales):
            for j in range(2):
                spread = scales[0, j:16:2, :].bitcast(I32).unsqueeze(1).to_broadcast([8, 8, scales.shape[2] // 4])
                nc.sync.dma_start(tile[j:P:2, :].bitcast(I32), spread)

        def shift_to_plane(name, dealt):
            plane = sb(name, list(dealt.shape), U8)
            nc.gpsimd.memset(plane[:].bitcast(I32), 0)
            nc.scalar.dma_start(plane[0:112, :].bitcast(I32), dealt[14:126, :].bitcast(I32))
            return plane

        warm = sb("warm", [P, 2], F32)
        nc.gpsimd.memset(warm[:, 0:1], 0.0)
        nc.scalar.activation(warm[:, 1:2], warm[:, 0:1], ACT.Sigmoid)

        d_scale_table = sb("d_scale_table", [P, G], U8)
        x_scale_table = sb("x_scale_table", [P, T], U8)
        nc.gpsimd.memset(x_scale_table[:].bitcast(I32), 0)
        k1_l = load_list("k1_l", k1)
        load_by_runs(d_scale_table[:], d_scales)
        two_l = load_list("two_l", two)
        n4_l = load_list("n4_l", n4)
        n3_l = load_list("n3_l", n3)
        x_word_table = sb("x_word_table", [P, T], I32)
        nc.sync.dma_start(x_word_table[:], x_words[0].rearrange("p n t -> p (n t)").bitcast(I32))
        d_word_table = sb("d_word_table", [P, G], I32)
        nc.sync.dma_start(d_word_table[:], d_words[0].rearrange("p n t -> p (n t)").bitcast(I32))
        load_plane(nc.sync, x_scale_table, x_scales)
        offs_l = load_list("offs_l", offs)

        w_words = sb("w_words", [P, 2, N], U16)
        for w, words in enumerate((w1_words, w2_words)):
            raw = sb(f"w_words_raw{w}", [P, 2 * N], U8)
            nc.sync.dma_start(raw[:].bitcast(I32), words[0].bitcast(I32))
            deal(nc.scalar.copy, w_words[:, w, :], raw[:].bitcast(U16), 8)

        key_scales_picked = sb("key_scales_picked", [P, H], U8)
        nc.vector.tensor_copy(key_scales_picked[:], d_scale_table[:].indirect(k1_l[:]))
        key_scales_dealt = sb("key_scales_dealt", [P, H], U8)
        deal(nc.vector.tensor_copy, key_scales_dealt[:], key_scales_picked[:], 16)
        key_plane = shift_to_plane("key_plane", key_scales_dealt)


        def pick_token_scales(name, lst):
            plane = sb(name, [P, S], U8)
            nc.vector.tensor_copy(plane[:], x_scale_table[:].indirect(lst[:]))
            return plane

        def pick_token_words(name, lst):
            words = sb(name, [P, S], U32)
            nc.vector.tensor_copy(words[:], x_word_table[:].bitcast(U32).indirect(lst[:]))
            return words

        two_plane = pick_token_scales("two_plane", two_l)
        key_words_picked = sb("key_words_picked", [P, H], U32)
        nc.vector.tensor_copy(key_words_picked[:], d_word_table[:].bitcast(U32).indirect(k1_l[:]))
        key_words = sb("key_words", [P, H], U32)
        deal(nc.vector.tensor_copy, key_words[:], key_words_picked[:], 4)
        two_words = pick_token_words("two_words", two_l)

        gn_t = sb("gn_t", [P, PACK], F32)
        nc.sync.dma_start(gn_t[:], gn.rearrange("(p t) o -> p (t o)", t=PACK))
        gn_16th = sb("gn_16th", [P, PACK], F32)
        nc.scalar.activation(gn_16th[:], gn_t[:], ACT.Copy, scale=0.0625)
        gm_t = sb("gm_t", [P, PACK], F32)
        nc.sync.dma_start(gm_t[:], gm.rearrange("(p t) o -> p (t o)", t=PACK))
        n2_l = load_list("n2_l", n2)
        n1_l = load_list("n1_l", n1)

        def scores(tag, words, plane):
            banks = []
            for t in range(PACK):
                bank = psum.tile([P, S], F32, name=f"{tag}{t}", tag=f"{tag}{t}")
                cols = slice(t * P, (t + 1) * P)
                nc.tensor.matmul_mx(
                    out=bank[:], lhsT=key_words[:, cols].bitcast(FP8X4), lhsT_scale=key_plane[:, cols],
                    rhs=words[:].bitcast(FP8X4), rhs_scale=plane[:], start=True, stop=True,
                )
                banks.append(bank)
            return banks

        b_banks = scores("left", two_words, two_plane)
        idx_plane = pick_token_scales("idx_plane", offs_l)
        idx_words = pick_token_words("idx_words", offs_l)
        a_banks = scores("right", idx_words, idx_plane)

        w_scales_raw = sb("w_scales_raw", [P, 2 * N], U8)
        w_scales_dealt = sb("w_scales_dealt", [P, 2 * N], U8)
        for w, scales in enumerate((w1_scales, w2_scales)):
            cols = slice(w * N, (w + 1) * N)
            load_by_runs(w_scales_raw[:, cols], scales)
            deal(nc.gpsimd.tensor_copy, w_scales_dealt[:, cols], w_scales_raw[:, cols], 16)
        w_plane = shift_to_plane("w_plane", w_scales_dealt)
        n5_l = load_list("n5_l", n5)
        n6_l = load_list("n6_l", n6)

        def window(name, width, engine):
            tile = sb(name, [P, width], F32)
            engine.memset(tile[:, S:], 0.0)
            return tile

        def weave(copy, woven, rows):
            planes = rows.shape[1]
            copy(woven.rearrange("p (c i t) -> p c t i", t=PACK, i=4)[:, :, :planes, :], rows.rearrange("p t (c i) -> p c t i", i=4))

        def quantise(name, woven, plane):
            words = sb(name, [P, plane.shape[1]], I32)
            nc.vector.quantize_mx(out=words[:].bitcast(FP8X4), scales=plane, in_=woven)
            return words

        ds = [window(f"ds{t}", 2 * W, nc.gpsimd) for t in range(PACK)]
        rows = [window(f"rows{t}", 2 * S, nc.vector) for t in range(PACK)]
        ra = [sb(f"ra{t}", [P, W], F32) for t in range(PACK)]
        z_rows = sb("z_rows", [P, PACK, S], F32)
        z2_rows = sb("z2_rows", [P, PACK - 1, S], BF16)
        z2_woven = sb("z2_woven", [P, PACK * S], BF16)

        def take_b(t):
            if t < 2:
                nc.scalar.activation(ds[t][:, :S], b_banks[t][:], ACT.Copy, scale=0.0625)
            else:
                nc.vector.tensor_scalar(ds[t][:, :S], b_banks[t][:], 0.0625, None, ALU.mult)

        def gate_columns(t):
            gate = sb(f"gate{t}", [P, W], F32)
            nc.scalar.activation(gate[:], ds[t][:].indirect(n4_l[:]), ACT.Sigmoid)
            nc.vector.tensor_tensor(ra[t][:], ds[t][:].indirect(n3_l[:]), gate[:], ALU.mult)

        def put_back(t):
            nc.scalar.activation(ds[t][:].indirect(n3_l[:]), ra[t][:], ACT.Copy)
            gain = gm_t[:, t : t + 1]
            if t < PACK - 1:
                nc.vector.tensor_scalar(z2_rows[:, t, :], ds[t][:, :S], gain, None, ALU.mult)
            else:
                nc.vector.tensor_scalar(z2_woven[:, t::PACK], ds[t][:, :S], gain, None, ALU.mult)

        def mix_neighbours(t):
            nc.scalar.activation(rows[t][:, :S], a_banks[t][:], ACT.Copy, scale=gn_16th[:, t : t + 1])
            second = sb(f"second{t}", [P, S], F32)
            for cols in halves:
                nc.vector.tensor_scalar(second[:, cols], rows[t][:].indirect(entries(n2_l, cols)), 0.75, 0.0, ALU.mult, ALU.add)
            for cols in halves:
                nc.vector.tensor_tensor(z_rows[:, t, cols], rows[t][:].indirect(entries(n1_l, cols)), second[:, cols], ALU.add)

        def finish_z(half):
            woven = sb(f"z_woven{half}", [P, PACK * HALF], BF16)
            weave(nc.scalar.copy, woven[:], z_rows[:, :, halves[half]])
            plane = sb(f"z_plane{half}", [P, HALF], U8)
            return quantise(f"z_words{half}", woven[:], plane[:]), plane

        for t in range(PACK):
            take_b(t)
        for t in range(PACK):
            gate_columns(t)
            mix_neighbours(t)
            if t > 0:
                put_back(t - 1)
        weave(nc.vector.tensor_copy, z2_woven[:], z2_rows[:])
        put_back(3)
        z2_plane = sb("z2_plane", [P, S], U8)
        z2_words = quantise("z2_words", z2_woven[:], z2_plane[:])
        z_halves = [finish_z(half) for half in range(2)]

        h_banks = [
            [psum.tile([P, HALF], F32, name=f"h{t}_{side}", tag=f"{side}{t}") for side in ("left", "right")] for t in range(PACK)
        ]

        def weights_pass(w, t, half, words, plane):
            keys = slice(t * P, (t + 1) * P)
            nc.tensor.matmul_mx(
                out=h_banks[t][half][:], lhsT=w_words[:, w, keys].bitcast(FP4X4), lhsT_scale=w_plane[:, w * N + t * P : w * N + (t + 1) * P],
                rhs=words.bitcast(FP8X4), rhs_scale=plane, start=w == 1, stop=w == 0,
            )

        for t in range(PACK):
            for half, cols in enumerate(halves):
                weights_pass(1, t, half, z2_words[:, cols], z2_plane[:, cols])
            for half, (words, plane) in enumerate(z_halves):
                weights_pass(0, t, half, words[:], plane[:])

        out_rows_hbm = out_0.rearrange("(p t) j -> p t j", t=PACK)
        out_words_hbm = out_1[0].rearrange("p n t -> p (n t)").bitcast(I32)
        out_plane = sb("out_plane", [P, S], U8)
        out_rows = sb("out_rows", [P, PACK, S], F32)
        for t in range(PACK):
            for half, cols in enumerate(halves):
                copy = nc.vector.tensor_copy if (t, half) in V_EVAC else nc.scalar.copy
                copy(rows[t][:, cols], h_banks[t][half][:])
            fifth = sb(f"fifth{t}", [P, S], F32)
            both = sb(f"both{t}", [P, S], F32)
            for cols in halves if t == 0 else (slice(0, S),):
                nc.scalar.activation(fifth[:, cols], rows[t][:].indirect(entries(n5_l, cols)), ACT.Copy)
            if t < PACK - 1:
                for cols in halves:
                    nc.vector.tensor_tensor(both[:, cols], rows[t][:].indirect(entries(n6_l, cols)), fifth[:, cols], ALU.add)
                for half, cols in enumerate(halves):
                    nc.vector.scalar_tensor_tensor(out_rows[:, t, cols], both[:, cols], 0.75, h_banks[t][half][:], ALU.mult, ALU.subtract)
            else:
                left, right = halves
                sixth = sb("sixth", [P, HALF], F32)
                nc.scalar.activation(sixth[:], rows[t][:].indirect(entries(n6_l, right)), ACT.Copy)
                nc.vector.tensor_tensor(both[:, left], rows[t][:].indirect(entries(n6_l, left)), fifth[:, left], ALU.add)
                nc.vector.scalar_tensor_tensor(both[:, right], fifth[:, right], 0.75, h_banks[t][1][:], ALU.mult, ALU.subtract)
                nc.vector.scalar_tensor_tensor(out_rows[:, t, left], both[:, left], 0.75, h_banks[t][0][:], ALU.mult, ALU.subtract)
                nc.vector.scalar_tensor_tensor(out_rows[:, t, right], sixth[:], 0.75, both[:, right], ALU.mult, ALU.add)
            nc.sync.dma_start(out_rows_hbm[:, t, :], out_rows[:, t, :])
        for half, copy in enumerate((nc.scalar.copy, nc.vector.tensor_copy)):
            cols = halves[half]
            out_woven = sb(f"out_woven{half}", [P, PACK * HALF], BF16)
            weave(copy, out_woven[:], out_rows[:, :, cols])
            out_words = quantise(f"out_words{half}", out_woven[:], out_plane[:, cols])
            nc.sync.dma_start(out_words_hbm[:, cols], out_words[:])
        for j in range(4):
            nc.scalar.dma_start(out_2[0, j:16:4, :].bitcast(I32), out_plane[j:P:32, :].bitcast(I32))
